import numpy as np
import ml_dtypes


def mxq(x, axis, fmt="e4m3"):
    dtype, down = {"e4m3": (ml_dtypes.float8_e4m3fn, 7), "e5m2": (ml_dtypes.float8_e5m2, 14)}[fmt]
    v = np.moveaxis(np.asarray(x, np.float32).astype(ml_dtypes.bfloat16).astype(np.float64), axis, -1)
    blocks = v.reshape(v.shape[:-1] + (-1, 32))
    amax = np.abs(blocks).max(-1, keepdims=True)
    byte = np.maximum(np.where(amax > 0, np.frexp(amax)[1] - 1 + 127, 0) - down, 1)
    scale = np.exp2(byte - 127.0)
    codes = (blocks / scale).astype(np.float32).astype(dtype).astype(np.float64)
    return np.moveaxis((codes * scale).reshape(v.shape), -1, axis)


WIDE = False


def mx_kscale(k):
    if not WIDE:
        return np.ones(k)
    levels = np.array([10, -10, 5, -5, 0])
    if k % 512:
        return np.exp2(np.random.permutation(np.resize(levels, k // 32))).repeat(32)
    a = np.empty((k // 512, 16))
    for p in range(k // 512):
        a[p, :8] = np.random.permutation(np.resize(levels, 8))
        for g in range(8):
            far = levels[np.abs(levels - a[p, g]) >= 10]
            a[p, g + 8] = far[np.random.randint(len(far))]
    return np.exp2(a.ravel()).repeat(32)


def f64(x):
    return np.asarray(x).astype(np.float64)


def striped(idx):
    return np.tile(idx.reshape(-1, 16).T, (8, 1)).astype(np.uint16)


def unstriped(offs):
    return offs[:16].T.reshape(-1).astype(np.int64)


def pack_weight(w):
    k, n = w.shape
    w = f64(np.asarray(w, np.float32).astype(ml_dtypes.bfloat16)).reshape(k // 32, 32, n)
    amax = np.abs(w).max(1)
    byte = np.clip(np.where(amax > 0, np.frexp(amax)[1] - 1 + 127 - 7, 1), 1, 254)
    scaled = (w * np.exp2(127.0 - byte)[:, None, :]).reshape(k, n).astype(np.float32)
    words = np.ascontiguousarray(scaled.reshape(k // 512, 128, 4, n).transpose(0, 1, 3, 2)).astype(ml_dtypes.float8_e4m3fn).view(np.uint8)
    return words, np.ascontiguousarray(byte.astype(np.uint8).reshape(k // 512, 16, n))


def unpack_weight(words, scales):
    g, p, n, _ = words.shape
    vals = np.ascontiguousarray(words).view(ml_dtypes.float8_e4m3fn).astype(np.float64) * np.repeat(np.exp2(scales.astype(np.float64) - 127.0), 8, axis=1)[..., None]
    return vals.transpose(0, 1, 3, 2).reshape(g * 512, n)


K, T, D, S, V, N = 512, 1024, 2, 512, 256, 128


def setup_inputs():
    n = np.random.standard_normal
    s = mx_kscale(K)[:, None]
    words, scales = pack_weight(n((K, N)) / np.sqrt(K) / s)
    return {
        "xT": (n((K, T)) * s / np.sqrt(D)).astype(ml_dtypes.bfloat16).astype(np.float32),
        "w_words": words,
        "w_scales": scales,
        "offs": striped(np.concatenate([np.random.permutation(T)[:V] for _ in range(D)])),
    }


def reference(xT, w_words, w_scales, offs):
    w = unpack_weight(w_words, w_scales)
    idx = unstriped(offs)
    x = sum(f64(xT)[:, idx[d * V:(d + 1) * V]] for d in range(D))
    return w.T @ mxq(x, 0, "e4m3")

@@ -1,0 +1,111 @@
+from contextlib import ExitStack
+
+import concourse.mybir as mybir
+
+K, T, D, V, N = 512, 1024, 2, 256, 128
+FLOPS = 2 * K * V * N
+
+F32 = mybir.dt.float32
+BF16 = mybir.dt.bfloat16
+I32 = mybir.dt.int32
+U32 = mybir.dt.uint32
+U16 = mybir.dt.uint16
+U8 = mybir.dt.uint8
+FP8X4 = mybir.dt.float8_e4m3fn_x4
+ADD = mybir.AluOpType.add
+
+P = 128
+HALF = V // 2
+CHUNKS = [(0, 0, 512, 512), (0, 512, 1024, 352), (1, 0, 512, 0), (1, 512, 768, 256), (1, 768, 1024, 160)]
+
+
+def tile_picked_hash_lin_none_sub_l_kernel(tc, xT, w_words, w_scales, offs, out):
+    nc = tc.nc
+    x_rows = xT.rearrange("(p u e) c -> p u e c", u=2, e=2)
+
+    with ExitStack() as ctx:
+        keep = ctx.enter_context(tc.tile_pool(name="keep", bufs=1))
+        psum = ctx.enter_context(tc.psum_pool(name="psum", bufs=1))
+
+        offsets = keep.tile([P, D * V // 16], U16, name="offsets")
+        w_codes = keep.tile([P, N], U32, name="w_codes", align_bytes=64)
+        w_plane = keep.tile([P, N], U8, name="w_plane", align_bytes=64)
+        warm_in = keep.tile([P, 8], F32, name="warm_in")
+        warm_out = keep.tile([P, 8], BF16, name="warm_out")
+        nc.vector.memset(w_plane[:].bitcast(U32), 0)
+        nc.vector.memset(warm_in[:], 0.0)
+        nc.scalar.copy(warm_out[:], warm_in[:])
+
+        raw = []
+        for i, (u, c0, c1, on_vector) in enumerate(CHUNKS):
+            chunk = keep.tile([P, 2, c1 - c0], F32, name="raw%d" % i)
+            nc.sync.dma_start(chunk[:], x_rows[:, u, :, c0:c1])
+            raw.append(chunk)
+            if i == 0:
+                nc.sync.dma_start(offsets[:], offs)
+        nc.sync.dma_start(w_codes[:].bitcast(I32), w_words[0].rearrange("p m r -> p (m r)").bitcast(I32))
+        for q in range(4):
+            nc.sync.dma_start(w_plane[32 * q : 32 * q + 4, :].bitcast(I32), w_scales[0, 4 * q : 4 * q + 4, :].bitcast(I32))
+
+        table = [keep.tile([P, T, 2], BF16, name="table%d" % u, align_bytes=64) for u in range(2)]
+        picked = [keep.tile([P, 2, V, 2], BF16, name="picked%d" % d, align_bytes=64) for d in range(D)]
+
+        def cast(i):
+            u, c0, c1, on_vector = CHUNKS[i]
+            src = raw[i][:].rearrange("p e c -> p c e")
+            if on_vector > 0:
+                nc.vector.tensor_copy(table[u][:, c0 : c0 + on_vector, :], src[:, 0:on_vector, :])
+            if on_vector < c1 - c0:
+                nc.scalar.copy(table[u][:, c0 + on_vector : c1, :], src[:, on_vector : c1 - c0, :])
+
+        def window(u):
+            return table[u][:].rearrange("p c e -> p (c e)").bitcast(U32)
+
+        def gather(u, d, v0, v1):
+            dst = picked[d][:, u, v0:v1, :].rearrange("p v e -> p (v e)").bitcast(U32)
+            cols = slice((d * V + v0) // 16, (d * V + v1) // 16)
+            nc.vector.tensor_copy(dst, window(u).indirect(offsets[:, cols]))
+
+        x_sum = [keep.tile([P, HALF, 2, 2], BF16, name="x_sum%d" % h, align_bytes=64) for h in range(2)]
+        x_codes = [keep.tile([P, HALF], U32, name="x_codes%d" % h, align_bytes=64) for h in range(2)]
+        x_plane = [keep.tile([P, HALF], U8, name="x_plane%d" % h, align_bytes=64) for h in range(2)]
+        acc = [psum.tile([P, HALF], F32, name="acc%d" % h) for h in range(2)]
+        result = [keep.tile([P, HALF], F32, name="result%d" % h) for h in range(2)]
+
+        def add(h):
+            vs = slice(h * HALF, (h + 1) * HALF)
+            a, b = (picked[d][:, :, vs, :].rearrange("p u v e -> p v u e") for d in range(D))
+            nc.vector.tensor_tensor(x_sum[h][:], a, b, ADD)
+
+        def quantize(h):
+            nc.vector.quantize_mx(out=x_codes[h][:].bitcast(FP8X4), scales=x_plane[h][:],
+                                  in_=x_sum[h][:].rearrange("p v u e -> p (v u e)"))
+
+        def finish(h):
+            nc.tensor.matmul_mx(out=acc[h][:], lhsT=w_codes[:].bitcast(FP8X4), lhsT_scale=w_plane[:],
+                                rhs=x_codes[h][:].bitcast(FP8X4), rhs_scale=x_plane[h][:], start=True, stop=True)
+            if h == 0:
+                nc.scalar.copy(result[h][:], acc[h][:])
+                nc.scalar.dma_start(out[:, h * HALF : (h + 1) * HALF], result[h][:])
+            else:
+                nc.vector.tensor_copy(result[h][:], acc[h][:])
+                nc.sync.dma_start(out[:, h * HALF : (h + 1) * HALF], result[h][:])
+
+        for i in range(len(CHUNKS)):
+            if CHUNKS[i][0] == 0:
+                cast(i)
+        gather(0, 0, 0, V)
+        gather(0, 1, 0, V)
+        for i in range(len(CHUNKS)):
+            if CHUNKS[i][0] == 1:
+                cast(i)
+        gather(1, 0, 0, HALF)
+        gather(1, 1, 0, HALF)
+        gather(1, 0, HALF, V)
+        add(0)
+        gather(1, 1, HALF, V)
+        quantize(0)
+        add(1)
+        finish(0)
+        quantize(1)
+        finish(1)

@@ -13,15 +13,16 @@ U16 = mybir.dt.uint16
 U8 = mybir.dt.uint8
 FP8X4 = mybir.dt.float8_e4m3fn_x4
 ADD = mybir.AluOpType.add
+COPY = mybir.ActivationFunctionType.Copy
 
 P = 128
 HALF = V // 2
-CHUNKS = [(0, 0, 512, 512), (0, 512, 1024, 352), (1, 0, 512, 0), (1, 512, 768, 256), (1, 768, 1024, 160)]
+CUTS = [[(0, 1024)], [(0, 1024)], [(0, 512), (512, 1024)], [(0, 1024)]]
 
 
 def tile_picked_hash_lin_none_sub_l_kernel(tc, xT, w_words, w_scales, offs, out):
     nc = tc.nc
-    x_rows = xT.rearrange("(p u e) c -> p u e c", u=2, e=2)
+    x_rows = xT.rearrange("(p t) c -> p t c", t=4)
 
     with ExitStack() as ctx:
         keep = ctx.enter_context(tc.tile_pool(name="keep", bufs=1))
@@ -34,37 +35,37 @@ def tile_picked_hash_lin_none_sub_l_kernel(tc, xT, w_words, w_scales, offs, out)
         warm_out = keep.tile([P, 8], BF16, name="warm_out")
         nc.vector.memset(w_plane[:].bitcast(U32), 0)
         nc.vector.memset(warm_in[:], 0.0)
-        nc.scalar.copy(warm_out[:], warm_in[:])
+        nc.scalar.activation(warm_out[:], warm_in[:], COPY)
 
-        raw = []
-        for i, (u, c0, c1, on_vector) in enumerate(CHUNKS):
-            chunk = keep.tile([P, 2, c1 - c0], F32, name="raw%d" % i)
-            nc.sync.dma_start(chunk[:], x_rows[:, u, :, c0:c1])
-            raw.append(chunk)
-            if i == 0:
+        plane = [keep.tile([P, T], F32, name="plane%d" % t, align_bytes=64) for t in range(4)]
+        for t in (1, 0, 3, 2):
+            for c0, c1 in CUTS[t]:
+                nc.sync.dma_start(plane[t][:, c0:c1], x_rows[:, t, c0:c1])
+            if t == 1:
                 nc.sync.dma_start(offsets[:], offs)
         nc.sync.dma_start(w_codes[:].bitcast(I32), w_words[0].rearrange("p m r -> p (m r)").bitcast(I32))
         for q in range(4):
             nc.sync.dma_start(w_plane[32 * q : 32 * q + 4, :].bitcast(I32), w_scales[0, 4 * q : 4 * q + 4, :].bitcast(I32))
 
-        table = [keep.tile([P, T, 2], BF16, name="table%d" % u, align_bytes=64) for u in range(2)]
+        narrow = [keep.tile([P, T], BF16, name="narrow%d" % u, align_bytes=64) for u in range(2)]
         picked = [keep.tile([P, 2, V, 2], BF16, name="picked%d" % d, align_bytes=64) for d in range(D)]
 
-        def cast(i):
-            u, c0, c1, on_vector = CHUNKS[i]
-            src = raw[i][:].rearrange("p e c -> p c e")
-            if on_vector > 0:
-                nc.vector.tensor_copy(table[u][:, c0 : c0 + on_vector, :], src[:, 0:on_vector, :])
-            if on_vector < c1 - c0:
-                nc.scalar.copy(table[u][:, c0 + on_vector : c1, :], src[:, on_vector : c1 - c0, :])
+        def entries(d, v0, v1):
+            return offsets[:, (d * V + v0) // 16 : (d * V + v1) // 16]
 
-        def window(u):
-            return table[u][:].rearrange("p c e -> p (c e)").bitcast(U32)
+        def gather_high(u, d):
+            dst = picked[d][:, u, :, :].rearrange("p v e -> p (v e)").bitcast(F32)
+            nc.vector.tensor_copy(dst, plane[2 * u + 1][:].indirect(entries(d, 0, V)))
 
-        def gather(u, d, v0, v1):
-            dst = picked[d][:, u, v0:v1, :].rearrange("p v e -> p (v e)").bitcast(U32)
-            cols = slice((d * V + v0) // 16, (d * V + v1) // 16)
-            nc.vector.tensor_copy(dst, window(u).indirect(offsets[:, cols]))
+        def gather_low(u, d, v0, v1):
+            nc.vector.tensor_copy(picked[d][:, u, v0:v1, 0], plane[2 * u][:].indirect(entries(d, v0, v1)))
+
+        def narrow_low(u):
+            for c0, c1 in CUTS[2 * u]:
+                nc.scalar.copy(narrow[u][:, c0:c1], plane[2 * u][:, c0:c1])
+
+        def gather_low_scalar(u, d, v0, v1):
+            nc.scalar.activation(picked[d][:, u, v0:v1, 0], narrow[u][:].indirect(entries(d, v0, v1)), COPY)
 
         x_sum = [keep.tile([P, HALF, 2, 2], BF16, name="x_sum%d" % h, align_bytes=64) for h in range(2)]
         x_codes = [keep.tile([P, HALF], U32, name="x_codes%d" % h, align_bytes=64) for h in range(2)]
@@ -91,21 +92,17 @@ def tile_picked_hash_lin_none_sub_l_kernel(tc, xT, w_words, w_scales, offs, out)
                 nc.vector.tensor_copy(result[h][:], acc[h][:])
                 nc.sync.dma_start(out[:, h * HALF : (h + 1) * HALF], result[h][:])
 
-        for i in range(len(CHUNKS)):
-            if CHUNKS[i][0] == 0:
-                cast(i)
-        gather(0, 0, 0, V)
-        gather(0, 1, 0, V)
-        for i in range(len(CHUNKS)):
-            if CHUNKS[i][0] == 1:
-                cast(i)
-        gather(1, 0, 0, HALF)
-        gather(1, 1, 0, HALF)
-        gather(1, 0, HALF, V)
+        for u in range(2):
+            gather_high(u, 1)
+            gather_high(u, 0)
+            narrow_low(u)
+            gather_low_scalar(u, 1, HALF, V)
+            gather_low(u, 1, 0, HALF)
+            gather_low(u, 0, 0, HALF)
+            gather_low(u, 0, HALF, V)
         add(0)
-        gather(1, 1, HALF, V)
-        quantize(0)
         add(1)
-        finish(0)
+        quantize(0)
         quantize(1)
+        finish(0)
         finish(1)

@@ -67,20 +67,20 @@ def tile_picked_hash_lin_none_sub_l_kernel(tc, xT, w_words, w_scales, offs, out)
         def gather_low_scalar(u, d, v0, v1):
             nc.scalar.activation(picked[d][:, u, v0:v1, 0], narrow[u][:].indirect(entries(d, v0, v1)), COPY)
 
-        x_sum = [keep.tile([P, HALF, 2, 2], BF16, name="x_sum%d" % h, align_bytes=64) for h in range(2)]
+        x_sum = keep.tile([P, V, 2, 2], BF16, name="x_sum", align_bytes=64)
         x_codes = [keep.tile([P, HALF], U32, name="x_codes%d" % h, align_bytes=64) for h in range(2)]
         x_plane = [keep.tile([P, HALF], U8, name="x_plane%d" % h, align_bytes=64) for h in range(2)]
         acc = [psum.tile([P, HALF], F32, name="acc%d" % h) for h in range(2)]
         result = [keep.tile([P, HALF], F32, name="result%d" % h) for h in range(2)]
 
-        def add(h):
-            vs = slice(h * HALF, (h + 1) * HALF)
+        def add(v0, v1):
+            vs = slice(v0, v1)
             a, b = (picked[d][:, :, vs, :].rearrange("p u v e -> p v u e") for d in range(D))
-            nc.vector.tensor_tensor(x_sum[h][:], a, b, ADD)
+            nc.vector.tensor_tensor(x_sum[:, vs, :, :], a, b, ADD)
 
         def quantize(h):
             nc.vector.quantize_mx(out=x_codes[h][:].bitcast(FP8X4), scales=x_plane[h][:],
-                                  in_=x_sum[h][:].rearrange("p v u e -> p (v u e)"))
+                                  in_=x_sum[:, h * HALF : (h + 1) * HALF, :, :].rearrange("p v u e -> p (v u e)"))
 
         def finish(h):
             nc.tensor.matmul_mx(out=acc[h][:], lhsT=w_codes[:].bitcast(FP8X4), lhsT_scale=w_plane[:],
@@ -100,8 +100,9 @@ def tile_picked_hash_lin_none_sub_l_kernel(tc, xT, w_words, w_scales, offs, out)
             gather_low(u, 1, 0, HALF)
             gather_low(u, 0, 0, HALF)
             gather_low(u, 0, HALF, V)
-        add(0)
-        add(1)
+        add(0, 112)
+        add(112, 160)
+        add(160, 256)
         quantize(0)
         quantize(1)
         finish(0)

@@ -87,7 +87,7 @@ def tile_picked_hash_lin_none_sub_l_kernel(tc, xT, w_words, w_scales, offs, out)
                                 rhs=x_codes[h][:].bitcast(FP8X4), rhs_scale=x_plane[h][:], start=True, stop=True)
             if h == 0:
                 nc.scalar.copy(result[h][:], acc[h][:])
-                nc.scalar.dma_start(out[:, h * HALF : (h + 1) * HALF], result[h][:])
+                nc.sync.dma_start(out[:, h * HALF : (h + 1) * HALF], result[h][:])
             else:
                 nc.vector.tensor_copy(result[h][:], acc[h][:])
                 nc.sync.dma_start(out[:, h * HALF : (h + 1) * HALF], result[h][:])

@@ -17,7 +17,7 @@ COPY = mybir.ActivationFunctionType.Copy
 
 P = 128
 HALF = V // 2
-CUTS = [[(0, 1024)], [(0, 1024)], [(0, 512), (512, 1024)], [(0, 1024)]]
+CUTS = [[(0, 512), (512, 1024)], [(0, 1024)], [(0, 384), (384, 768), (768, 1024)], [(0, 1024)]]
 
 
 def tile_picked_hash_lin_none_sub_l_kernel(tc, xT, w_words, w_scales, offs, out):
@@ -48,24 +48,27 @@ def tile_picked_hash_lin_none_sub_l_kernel(tc, xT, w_words, w_scales, offs, out)
             nc.sync.dma_start(w_plane[32 * q : 32 * q + 4, :].bitcast(I32), w_scales[0, 4 * q : 4 * q + 4, :].bitcast(I32))
 
         narrow = [keep.tile([P, T], BF16, name="narrow%d" % u, align_bytes=64) for u in range(2)]
-        picked = [keep.tile([P, 2, V, 2], BF16, name="picked%d" % d, align_bytes=64) for d in range(D)]
+        picked = [keep.tile([P, 2 * V * 2], BF16, name="picked%d" % d, align_bytes=64) for d in range(D)]
 
         def entries(d, v0, v1):
             return offsets[:, (d * V + v0) // 16 : (d * V + v1) // 16]
 
         def gather_high(u, d):
-            dst = picked[d][:, u, :, :].rearrange("p v e -> p (v e)").bitcast(F32)
+            dst = picked[d][:, 2 * V * u : 2 * V * (u + 1)].bitcast(F32)
             nc.vector.tensor_copy(dst, plane[2 * u + 1][:].indirect(entries(d, 0, V)))
 
+        def low(u, d, v0, v1):
+            return picked[d][:, 2 * (V * u + v0) : 2 * (V * u + v1) : 2]
+
         def gather_low(u, d, v0, v1):
-            nc.vector.tensor_copy(picked[d][:, u, v0:v1, 0], plane[2 * u][:].indirect(entries(d, v0, v1)))
+            nc.vector.tensor_copy(low(u, d, v0, v1), plane[2 * u][:].indirect(entries(d, v0, v1)))
 
         def narrow_low(u):
             for c0, c1 in CUTS[2 * u]:
                 nc.scalar.copy(narrow[u][:, c0:c1], plane[2 * u][:, c0:c1])
 
         def gather_low_scalar(u, d, v0, v1):
-            nc.scalar.activation(picked[d][:, u, v0:v1, 0], narrow[u][:].indirect(entries(d, v0, v1)), COPY)
+            nc.scalar.activation(low(u, d, v0, v1), narrow[u][:].indirect(entries(d, v0, v1)), COPY)
 
         x_sum = keep.tile([P, V, 2, 2], BF16, name="x_sum", align_bytes=64)
         x_codes = [keep.tile([P, HALF], U32, name="x_codes%d" % h, align_bytes=64) for h in range(2)]
@@ -75,7 +78,7 @@ def tile_picked_hash_lin_none_sub_l_kernel(tc, xT, w_words, w_scales, offs, out)
 
         def add(v0, v1):
             vs = slice(v0, v1)
-            a, b = (picked[d][:, :, vs, :].rearrange("p u v e -> p v u e") for d in range(D))
+            a, b = (picked[d][:].rearrange("p (u v e) -> p v u e", u=2, e=2)[:, vs, :, :] for d in range(D))
             nc.vector.tensor_tensor(x_sum[:, vs, :, :], a, b, ADD)
 
         def quantize(h):
@@ -92,17 +95,20 @@ def tile_picked_hash_lin_none_sub_l_kernel(tc, xT, w_words, w_scales, offs, out)
                 nc.vector.tensor_copy(result[h][:], acc[h][:])
                 nc.sync.dma_start(out[:, h * HALF : (h + 1) * HALF], result[h][:])
 
-        for u in range(2):
-            gather_high(u, 1)
-            gather_high(u, 0)
-            narrow_low(u)
-            gather_low_scalar(u, 1, HALF, V)
-            gather_low(u, 1, 0, HALF)
-            gather_low(u, 0, 0, HALF)
-            gather_low(u, 0, HALF, V)
-        add(0, 112)
-        add(112, 160)
-        add(160, 256)
+        gather_high(0, 1)
+        gather_high(0, 0)
+        narrow_low(0)
+        gather_low_scalar(0, 1, 0, V)
+        gather_low(0, 0, 0, V)
+        gather_high(1, 1)
+        gather_high(1, 0)
+        narrow_low(1)
+        gather_low_scalar(1, 1, HALF, V)
+        gather_low_scalar(1, 0, HALF, V)
+        gather_low(1, 1, 0, HALF)
+        gather_low(1, 0, 0, HALF)
+        add(0, HALF)
+        add(HALF, V)
         quantize(0)
         quantize(1)
         finish(0)

@@ -16,8 +16,10 @@ ADD = mybir.AluOpType.add
 COPY = mybir.ActivationFunctionType.Copy
 
 P = 128
+S = D * V
 HALF = V // 2
-CUTS = [[(0, 512), (512, 1024)], [(0, 1024)], [(0, 384), (384, 768), (768, 1024)], [(0, 1024)]]
+CUTS = [[(0, 512), (512, 1024)], [(0, 1024)], [(0, 512), (512, 1024)], [(0, 1024)]]
+PARTS = [(0, 128), (128, 256)]
 
 
 def tile_picked_hash_lin_none_sub_l_kernel(tc, xT, w_words, w_scales, offs, out):
@@ -28,7 +30,7 @@ def tile_picked_hash_lin_none_sub_l_kernel(tc, xT, w_words, w_scales, offs, out)
         keep = ctx.enter_context(tc.tile_pool(name="keep", bufs=1))
         psum = ctx.enter_context(tc.psum_pool(name="psum", bufs=1))
 
-        offsets = keep.tile([P, D * V // 16], U16, name="offsets")
+        offsets = keep.tile([P, S // 16], U16, name="offsets")
         w_codes = keep.tile([P, N], U32, name="w_codes", align_bytes=64)
         w_plane = keep.tile([P, N], U8, name="w_plane", align_bytes=64)
         warm_in = keep.tile([P, 8], F32, name="warm_in")
@@ -50,66 +52,64 @@ def tile_picked_hash_lin_none_sub_l_kernel(tc, xT, w_words, w_scales, offs, out)
         narrow = [keep.tile([P, T], BF16, name="narrow%d" % u, align_bytes=64) for u in range(2)]
         picked = [keep.tile([P, 2 * V * 2], BF16, name="picked%d" % d, align_bytes=64) for d in range(D)]
 
-        def entries(d, v0, v1):
-            return offsets[:, (d * V + v0) // 16 : (d * V + v1) // 16]
+        def entries(j0, j1):
+            return offsets[:, j0 // 16 : j1 // 16]
 
-        def gather_high(u, d):
-            dst = picked[d][:, 2 * V * u : 2 * V * (u + 1)].bitcast(F32)
-            nc.vector.tensor_copy(dst, plane[2 * u + 1][:].indirect(entries(d, 0, V)))
+        def words(u, j0, j1):
+            d = j0 // V
+            return picked[d][:, 2 * (V * (u - d) + j0) : 2 * (V * (u - d) + j1)]
 
-        def low(u, d, v0, v1):
-            return picked[d][:, 2 * (V * u + v0) : 2 * (V * u + v1) : 2]
+        def gather_high(u, j0, j1):
+            nc.vector.tensor_copy(words(u, j0, j1).bitcast(F32), plane[2 * u + 1][:].indirect(entries(j0, j1)))
 
-        def gather_low(u, d, v0, v1):
-            nc.vector.tensor_copy(low(u, d, v0, v1), plane[2 * u][:].indirect(entries(d, v0, v1)))
+        def gather_low(u, j0, j1):
+            nc.vector.tensor_copy(words(u, j0, j1)[:, ::2], plane[2 * u][:].indirect(entries(j0, j1)))
 
         def narrow_low(u):
             for c0, c1 in CUTS[2 * u]:
                 nc.scalar.copy(narrow[u][:, c0:c1], plane[2 * u][:, c0:c1])
 
-        def gather_low_scalar(u, d, v0, v1):
-            nc.scalar.activation(low(u, d, v0, v1), narrow[u][:].indirect(entries(d, v0, v1)), COPY)
+        def gather_low_scalar(u, j0, j1):
+            nc.scalar.activation(words(u, j0, j1)[:, ::2], narrow[u][:].indirect(entries(j0, j1)), COPY)
 
-        x_sum = keep.tile([P, V, 2, 2], BF16, name="x_sum", align_bytes=64)
-        x_codes = [keep.tile([P, HALF], U32, name="x_codes%d" % h, align_bytes=64) for h in range(2)]
-        x_plane = [keep.tile([P, HALF], U8, name="x_plane%d" % h, align_bytes=64) for h in range(2)]
-        acc = [psum.tile([P, HALF], F32, name="acc%d" % h) for h in range(2)]
-        result = [keep.tile([P, HALF], F32, name="result%d" % h) for h in range(2)]
+        x_sum = keep.tile([P, 4 * V], BF16, name="x_sum", align_bytes=64)
+        x_codes = [keep.tile([P, v1 - v0], U32, name="x_codes%d" % v0, align_bytes=64) for v0, v1 in PARTS]
+        x_plane = [keep.tile([P, v1 - v0], U8, name="x_plane%d" % v0, align_bytes=64) for v0, v1 in PARTS]
+        acc = [psum.tile([P, v1 - v0], F32, name="acc%d" % v0) for v0, v1 in PARTS]
+        result = [keep.tile([P, v1 - v0], F32, name="result%d" % v0) for v0, v1 in PARTS]
 
         def add(v0, v1):
-            vs = slice(v0, v1)
-            a, b = (picked[d][:].rearrange("p (u v e) -> p v u e", u=2, e=2)[:, vs, :, :] for d in range(D))
-            nc.vector.tensor_tensor(x_sum[:, vs, :, :], a, b, ADD)
+            by_piece = [picked[d][:].rearrange("p (u v e) -> p v u e", u=2, e=2) for d in range(D)]
+            nc.vector.tensor_tensor(x_sum[:, 4 * v0 : 4 * v1].rearrange("p (v u e) -> p v u e", u=2, e=2),
+                                    by_piece[0][:, v0:v1], by_piece[1][:, v0:v1], ADD)
 
         def quantize(h):
-            nc.vector.quantize_mx(out=x_codes[h][:].bitcast(FP8X4), scales=x_plane[h][:],
-                                  in_=x_sum[:, h * HALF : (h + 1) * HALF, :, :].rearrange("p v u e -> p (v u e)"))
+            v0, v1 = PARTS[h]
+            nc.vector.quantize_mx(out=x_codes[h][:].bitcast(FP8X4), scales=x_plane[h][:], in_=x_sum[:, 4 * v0 : 4 * v1])
 
-        def finish(h):
+        def finish(h, leave, queue):
+            v0, v1 = PARTS[h]
             nc.tensor.matmul_mx(out=acc[h][:], lhsT=w_codes[:].bitcast(FP8X4), lhsT_scale=w_plane[:],
                                 rhs=x_codes[h][:].bitcast(FP8X4), rhs_scale=x_plane[h][:], start=True, stop=True)
-            if h == 0:
-                nc.scalar.copy(result[h][:], acc[h][:])
-                nc.sync.dma_start(out[:, h * HALF : (h + 1) * HALF], result[h][:])
-            else:
-                nc.vector.tensor_copy(result[h][:], acc[h][:])
-                nc.sync.dma_start(out[:, h * HALF : (h + 1) * HALF], result[h][:])
+            leave(result[h][:], acc[h][:])
+            queue.dma_start(out[:, v0:v1], result[h][:])
 
-        gather_high(0, 1)
-        gather_high(0, 0)
+        gather_high(0, 0, V)
+        gather_high(0, V, S)
         narrow_low(0)
-        gather_low_scalar(0, 1, 0, V)
-        gather_low(0, 0, 0, V)
-        gather_high(1, 1)
-        gather_high(1, 0)
+        gather_low_scalar(0, V, S)
+        gather_low(0, 0, V)
+        gather_high(1, V, S)
+        gather_high(1, 0, V)
         narrow_low(1)
-        gather_low_scalar(1, 1, HALF, V)
-        gather_low_scalar(1, 0, HALF, V)
-        gather_low(1, 1, 0, HALF)
-        gather_low(1, 0, 0, HALF)
-        add(0, HALF)
-        add(HALF, V)
+        gather_low_scalar(1, V + HALF, S)
+        gather_low(1, V, V + HALF)
+        gather_low(1, 0, HALF)
+        gather_low(1, HALF, V)
+        add(0, 112)
+        add(112, 160)
+        add(160, V)
         quantize(0)
         quantize(1)
-        finish(0)
-        finish(1)
+        finish(0, nc.scalar.copy, nc.sync)
+        finish(1, nc.vector.tensor_copy, nc.sync)

@@ -49,7 +49,7 @@ def tile_picked_hash_lin_none_sub_l_kernel(tc, xT, w_words, w_scales, offs, out)
         for q in range(4):
             nc.sync.dma_start(w_plane[32 * q : 32 * q + 4, :].bitcast(I32), w_scales[0, 4 * q : 4 * q + 4, :].bitcast(I32))
 
-        narrow = [keep.tile([P, T], BF16, name="narrow%d" % u, align_bytes=64) for u in range(2)]
+        narrow = [keep.tile([P, T], BF16, name="narrow%d" % u, tag="narrow%d" % u, align_bytes=64) for u in range(2)]
         picked = [keep.tile([P, 2 * V * 2], BF16, name="picked%d" % d, align_bytes=64) for d in range(D)]
 
         def entries(j0, j1):
@@ -73,7 +73,7 @@ def tile_picked_hash_lin_none_sub_l_kernel(tc, xT, w_words, w_scales, offs, out)
             nc.scalar.activation(words(u, j0, j1)[:, ::2], narrow[u][:].indirect(entries(j0, j1)), COPY)
 
         x_sum = keep.tile([P, 4 * V], BF16, name="x_sum", align_bytes=64)
-        x_codes = [keep.tile([P, v1 - v0], U32, name="x_codes%d" % v0, align_bytes=64) for v0, v1 in PARTS]
+        x_codes = []
         x_plane = [keep.tile([P, v1 - v0], U8, name="x_plane%d" % v0, align_bytes=64) for v0, v1 in PARTS]
         acc = [psum.tile([P, v1 - v0], F32, name="acc%d" % v0) for v0, v1 in PARTS]
         result = [keep.tile([P, v1 - v0], F32, name="result%d" % v0) for v0, v1 in PARTS]
@@ -85,6 +85,7 @@ def tile_picked_hash_lin_none_sub_l_kernel(tc, xT, w_words, w_scales, offs, out)
 
         def quantize(h):
             v0, v1 = PARTS[h]
+            x_codes.append(keep.tile([P, v1 - v0], U32, name="x_codes%d" % h, tag="narrow%d" % (1 - h), align_bytes=64))
             nc.vector.quantize_mx(out=x_codes[h][:].bitcast(FP8X4), scales=x_plane[h][:], in_=x_sum[:, 4 * v0 : 4 * v1])
 
         def finish(h, leave, queue):
@@ -106,9 +107,8 @@ def tile_picked_hash_lin_none_sub_l_kernel(tc, xT, w_words, w_scales, offs, out)
         gather_low(1, V, V + HALF)
         gather_low(1, 0, HALF)
         gather_low(1, HALF, V)
-        add(0, 112)
-        add(112, 160)
-        add(160, V)
+        add(0, HALF)
+        add(HALF, V)
         quantize(0)
         quantize(1)
         finish(0, nc.scalar.copy, nc.sync)

@@ -30,16 +30,16 @@ def tile_picked_hash_lin_none_sub_l_kernel(tc, xT, w_words, w_scales, offs, out)
         keep = ctx.enter_context(tc.tile_pool(name="keep", bufs=1))
         psum = ctx.enter_context(tc.psum_pool(name="psum", bufs=1))
 
-        offsets = keep.tile([P, S // 16], U16, name="offsets")
-        w_codes = keep.tile([P, N], U32, name="w_codes", align_bytes=64)
-        w_plane = keep.tile([P, N], U8, name="w_plane", align_bytes=64)
+        offsets = keep.tile([P, S // 16], U16, name="offsets", align_bytes=256)
+        w_codes = keep.tile([P, N], U32, name="w_codes", align_bytes=256)
+        w_plane = keep.tile([P, N], U8, name="w_plane", align_bytes=256)
         warm_in = keep.tile([P, 8], F32, name="warm_in")
         warm_out = keep.tile([P, 8], BF16, name="warm_out")
         nc.vector.memset(w_plane[:].bitcast(U32), 0)
         nc.vector.memset(warm_in[:], 0.0)
         nc.scalar.activation(warm_out[:], warm_in[:], COPY)
 
-        plane = [keep.tile([P, T], F32, name="plane%d" % t, align_bytes=64) for t in range(4)]
+        plane = [keep.tile([P, T], F32, name="plane%d" % t, align_bytes=256) for t in range(4)]
         for t in (1, 0, 3, 2):
             for c0, c1 in CUTS[t]:
                 nc.sync.dma_start(plane[t][:, c0:c1], x_rows[:, t, c0:c1])
@@ -49,8 +49,8 @@ def tile_picked_hash_lin_none_sub_l_kernel(tc, xT, w_words, w_scales, offs, out)
         for q in range(4):
             nc.sync.dma_start(w_plane[32 * q : 32 * q + 4, :].bitcast(I32), w_scales[0, 4 * q : 4 * q + 4, :].bitcast(I32))
 
-        narrow = [keep.tile([P, T], BF16, name="narrow%d" % u, tag="narrow%d" % u, align_bytes=64) for u in range(2)]
-        picked = [keep.tile([P, 2 * V * 2], BF16, name="picked%d" % d, align_bytes=64) for d in range(D)]
+        narrow = [keep.tile([P, T], BF16, name="narrow%d" % u, tag="narrow%d" % u, align_bytes=256) for u in range(2)]
+        picked = [keep.tile([P, 2 * V * 2], BF16, name="picked%d" % d, align_bytes=256) for d in range(D)]
 
         def entries(j0, j1):
             return offsets[:, j0 // 16 : j1 // 16]
@@ -72,11 +72,11 @@ def tile_picked_hash_lin_none_sub_l_kernel(tc, xT, w_words, w_scales, offs, out)
         def gather_low_scalar(u, j0, j1):
             nc.scalar.activation(words(u, j0, j1)[:, ::2], narrow[u][:].indirect(entries(j0, j1)), COPY)
 
-        x_sum = keep.tile([P, 4 * V], BF16, name="x_sum", align_bytes=64)
+        x_sum = keep.tile([P, 4 * V], BF16, name="x_sum", align_bytes=256)
         x_codes = []
-        x_plane = [keep.tile([P, v1 - v0], U8, name="x_plane%d" % v0, align_bytes=64) for v0, v1 in PARTS]
+        x_plane = [keep.tile([P, v1 - v0], U8, name="x_plane%d" % v0, align_bytes=256) for v0, v1 in PARTS]
         acc = [psum.tile([P, v1 - v0], F32, name="acc%d" % v0) for v0, v1 in PARTS]
-        result = [keep.tile([P, v1 - v0], F32, name="result%d" % v0) for v0, v1 in PARTS]
+        result = [keep.tile([P, v1 - v0], F32, name="result%d" % v0, align_bytes=256) for v0, v1 in PARTS]
 
         def add(v0, v1):
             by_piece = [picked[d][:].rearrange("p (u v e) -> p v u e", u=2, e=2) for d in range(D)]
@@ -85,7 +85,7 @@ def tile_picked_hash_lin_none_sub_l_kernel(tc, xT, w_words, w_scales, offs, out)
 
         def quantize(h):
             v0, v1 = PARTS[h]
-            x_codes.append(keep.tile([P, v1 - v0], U32, name="x_codes%d" % h, tag="narrow%d" % (1 - h), align_bytes=64))
+            x_codes.append(keep.tile([P, v1 - v0], U32, name="x_codes%d" % h, tag="narrow%d" % (1 - h), align_bytes=256))
             nc.vector.quantize_mx(out=x_codes[h][:].bitcast(FP8X4), scales=x_plane[h][:], in_=x_sum[:, 4 * v0 : 4 * v1])
 
         def finish(h, leave, queue):

@@ -33,13 +33,11 @@ def tile_picked_hash_lin_none_sub_l_kernel(tc, xT, w_words, w_scales, offs, out)
         offsets = keep.tile([P, S // 16], U16, name="offsets", align_bytes=256)
         w_codes = keep.tile([P, N], U32, name="w_codes", align_bytes=256)
         w_plane = keep.tile([P, N], U8, name="w_plane", align_bytes=256)
-        warm_in = keep.tile([P, 8], F32, name="warm_in")
         warm_out = keep.tile([P, 8], BF16, name="warm_out")
         nc.vector.memset(w_plane[:].bitcast(U32), 0)
-        nc.vector.memset(warm_in[:], 0.0)
-        nc.scalar.activation(warm_out[:], warm_in[:], COPY)
+        nc.scalar.activation(warm_out[:], w_plane[:, 0:32].bitcast(F32), COPY)
 
-        plane = [keep.tile([P, T], F32, name="plane%d" % t, align_bytes=256) for t in range(4)]
+        plane = [keep.tile([P, T], F32, name="plane%d" % t, align_bytes=4096) for t in range(4)]
         for t in (1, 0, 3, 2):
             for c0, c1 in CUTS[t]:
                 nc.sync.dma_start(plane[t][:, c0:c1], x_rows[:, t, c0:c1])

@@ -43,9 +43,9 @@ def tile_picked_hash_lin_none_sub_l_kernel(tc, xT, w_words, w_scales, offs, out)
                 nc.sync.dma_start(plane[t][:, c0:c1], x_rows[:, t, c0:c1])
             if t == 1:
                 nc.sync.dma_start(offsets[:], offs)
-        nc.sync.dma_start(w_codes[:].bitcast(I32), w_words[0].rearrange("p m r -> p (m r)").bitcast(I32))
         for q in range(4):
             nc.sync.dma_start(w_plane[32 * q : 32 * q + 4, :].bitcast(I32), w_scales[0, 4 * q : 4 * q + 4, :].bitcast(I32))
+        nc.sync.dma_start(w_codes[:].bitcast(I32), w_words[0].rearrange("p m r -> p (m r)").bitcast(I32))
 
         narrow = [keep.tile([P, T], BF16, name="narrow%d" % u, tag="narrow%d" % u, align_bytes=256) for u in range(2)]
         picked = [keep.tile([P, 2 * V * 2], BF16, name="picked%d" % d, align_bytes=256) for d in range(D)]

@@ -18,8 +18,7 @@ COPY = mybir.ActivationFunctionType.Copy
 P = 128
 S = D * V
 HALF = V // 2
-CUTS = [[(0, 512), (512, 1024)], [(0, 1024)], [(0, 512), (512, 1024)], [(0, 1024)]]
-PARTS = [(0, 128), (128, 256)]
+HALVES = [(0, HALF), (HALF, V)]
 
 
 def tile_picked_hash_lin_none_sub_l_kernel(tc, xT, w_words, w_scales, offs, out):
@@ -38,76 +37,65 @@ def tile_picked_hash_lin_none_sub_l_kernel(tc, xT, w_words, w_scales, offs, out)
         nc.scalar.activation(warm_out[:], w_plane[:, 0:32].bitcast(F32), COPY)
 
         plane = [keep.tile([P, T], F32, name="plane%d" % t, align_bytes=4096) for t in range(4)]
-        for t in (1, 0, 3, 2):
-            for c0, c1 in CUTS[t]:
-                nc.sync.dma_start(plane[t][:, c0:c1], x_rows[:, t, c0:c1])
-            if t == 1:
+        for t in (0, 2, 1, 3):
+            nc.sync.dma_start(plane[t][:], x_rows[:, t, :])
+            if t == 0:
                 nc.sync.dma_start(offsets[:], offs)
         for q in range(4):
             nc.sync.dma_start(w_plane[32 * q : 32 * q + 4, :].bitcast(I32), w_scales[0, 4 * q : 4 * q + 4, :].bitcast(I32))
         nc.sync.dma_start(w_codes[:].bitcast(I32), w_words[0].rearrange("p m r -> p (m r)").bitcast(I32))
 
-        narrow = [keep.tile([P, T], BF16, name="narrow%d" % u, tag="narrow%d" % u, align_bytes=256) for u in range(2)]
-        picked = [keep.tile([P, 2 * V * 2], BF16, name="picked%d" % d, align_bytes=256) for d in range(D)]
+        def entries(d, v0, v1):
+            return offsets[:, (V * d + v0) // 16 : (V * d + v1) // 16]
 
-        def entries(j0, j1):
-            return offsets[:, j0 // 16 : j1 // 16]
+        even = [[keep.tile([P, V], F32, name="even%d_%d" % (u, d), align_bytes=256) for d in range(D)] for u in range(2)]
+        left = keep.tile([P, 2 * 2 * V], BF16, name="left", align_bytes=256)
+        right = keep.tile([P, 2 * V], F32, name="right", align_bytes=256)
 
-        def words(u, j0, j1):
-            d = j0 // V
-            return picked[d][:, 2 * (V * (u - d) + j0) : 2 * (V * (u - d) + j1)]
+        def gather_even(u):
+            nc.vector.tensor_copy(even[u][0][:], plane[2 * u][:].indirect(entries(0, 0, V)))
+            nc.scalar.activation(even[u][1][:], plane[2 * u][:].indirect(entries(1, 0, V)), COPY)
 
-        def gather_high(u, j0, j1):
-            nc.vector.tensor_copy(words(u, j0, j1).bitcast(F32), plane[2 * u + 1][:].indirect(entries(j0, j1)))
+        def sum_even(u):
+            halves = [even[u][d][:].bitcast(BF16)[:, 1 : 2 * V] for d in range(D)]
+            nc.vector.tensor_tensor(left[:, 2 * V * u : 2 * V * (u + 1) - 1], halves[0], halves[1], ADD)
 
-        def gather_low(u, j0, j1):
-            nc.vector.tensor_copy(words(u, j0, j1)[:, ::2], plane[2 * u][:].indirect(entries(j0, j1)))
-
-        def narrow_low(u):
-            for c0, c1 in CUTS[2 * u]:
-                nc.scalar.copy(narrow[u][:, c0:c1], plane[2 * u][:, c0:c1])
-
-        def gather_low_scalar(u, j0, j1):
-            nc.scalar.activation(words(u, j0, j1)[:, ::2], narrow[u][:].indirect(entries(j0, j1)), COPY)
+        def gather_odd(u, v0, v1):
+            upper = left[:, 2 * (V * u + v0) + 1 : 2 * (V * u + v1) : 2]
+            nc.vector.tensor_copy(upper, plane[2 * u + 1][:].indirect(entries(0, v0, v1)))
+            nc.scalar.activation(right[:, V * u + v0 : V * u + v1], plane[2 * u + 1][:].indirect(entries(1, v0, v1)), COPY)
 
         x_sum = keep.tile([P, 4 * V], BF16, name="x_sum", align_bytes=256)
-        x_codes = []
-        x_plane = [keep.tile([P, v1 - v0], U8, name="x_plane%d" % v0, align_bytes=256) for v0, v1 in PARTS]
-        acc = [psum.tile([P, v1 - v0], F32, name="acc%d" % v0) for v0, v1 in PARTS]
-        result = [keep.tile([P, v1 - v0], F32, name="result%d" % v0, align_bytes=256) for v0, v1 in PARTS]
+        x_codes = [keep.tile([P, HALF], U32, name="x_codes%d" % h, align_bytes=256) for h in range(2)]
+        x_plane = [keep.tile([P, HALF], U8, name="x_plane%d" % h, align_bytes=256) for h in range(2)]
+        acc = [psum.tile([P, HALF], F32, name="acc%d" % h) for h in range(2)]
+        result = [keep.tile([P, HALF], F32, name="result%d" % h, align_bytes=256) for h in range(2)]
 
         def add(v0, v1):
-            by_piece = [picked[d][:].rearrange("p (u v e) -> p v u e", u=2, e=2) for d in range(D)]
+            sides = [side.rearrange("p (u v e) -> p v u e", u=2, e=2) for side in (left[:], right[:].bitcast(BF16))]
             nc.vector.tensor_tensor(x_sum[:, 4 * v0 : 4 * v1].rearrange("p (v u e) -> p v u e", u=2, e=2),
-                                    by_piece[0][:, v0:v1], by_piece[1][:, v0:v1], ADD)
+                                    sides[0][:, v0:v1], sides[1][:, v0:v1], ADD)
 
         def quantize(h):
-            v0, v1 = PARTS[h]
-            x_codes.append(keep.tile([P, v1 - v0], U32, name="x_codes%d" % h, tag="narrow%d" % (1 - h), align_bytes=256))
+            v0, v1 = HALVES[h]
             nc.vector.quantize_mx(out=x_codes[h][:].bitcast(FP8X4), scales=x_plane[h][:], in_=x_sum[:, 4 * v0 : 4 * v1])
 
-        def finish(h, leave, queue):
-            v0, v1 = PARTS[h]
+        def finish(h, leave):
+            v0, v1 = HALVES[h]
             nc.tensor.matmul_mx(out=acc[h][:], lhsT=w_codes[:].bitcast(FP8X4), lhsT_scale=w_plane[:],
                                 rhs=x_codes[h][:].bitcast(FP8X4), rhs_scale=x_plane[h][:], start=True, stop=True)
             leave(result[h][:], acc[h][:])
-            queue.dma_start(out[:, v0:v1], result[h][:])
+            nc.sync.dma_start(out[:, v0:v1], result[h][:])
 
-        gather_high(0, 0, V)
-        gather_high(0, V, S)
-        narrow_low(0)
-        gather_low_scalar(0, V, S)
-        gather_low(0, 0, V)
-        gather_high(1, V, S)
-        gather_high(1, 0, V)
-        narrow_low(1)
-        gather_low_scalar(1, V + HALF, S)
-        gather_low(1, V, V + HALF)
-        gather_low(1, 0, HALF)
-        gather_low(1, HALF, V)
-        add(0, HALF)
-        add(HALF, V)
+        for u in range(2):
+            gather_even(u)
+            sum_even(u)
+        gather_odd(0, 0, V)
+        for v0, v1 in HALVES:
+            gather_odd(1, v0, v1)
+        for v0, v1 in HALVES:
+            add(v0, v1)
         quantize(0)
         quantize(1)
-        finish(0, nc.scalar.copy, nc.sync)
-        finish(1, nc.vector.tensor_copy, nc.sync)
+        finish(0, nc.scalar.copy)
+        finish(1, nc.vector.tensor_copy)

@@ -33,14 +33,16 @@ def tile_picked_hash_lin_none_sub_l_kernel(tc, xT, w_words, w_scales, offs, out)
         w_codes = keep.tile([P, N], U32, name="w_codes", align_bytes=256)
         w_plane = keep.tile([P, N], U8, name="w_plane", align_bytes=256)
         warm_out = keep.tile([P, 8], BF16, name="warm_out")
-        nc.vector.memset(w_plane[:].bitcast(U32), 0)
-        nc.scalar.activation(warm_out[:], w_plane[:, 0:32].bitcast(F32), COPY)
-
         plane = [keep.tile([P, T], F32, name="plane%d" % t, align_bytes=4096) for t in range(4)]
-        for t in (0, 2, 1, 3):
-            nc.sync.dma_start(plane[t][:], x_rows[:, t, :])
+        for t in (0, 2, 1):
+            nc.sync.dma_start(plane[t][:, : T // 2], x_rows[:, t, : T // 2])
+            nc.scalar.dma_start(plane[t][:, T // 2 :], x_rows[:, t, T // 2 :])
             if t == 0:
                 nc.sync.dma_start(offsets[:], offs)
+        nc.sync.dma_start(plane[3][:], x_rows[:, 3, :])
+
+        nc.vector.memset(w_plane[:].bitcast(U32), 0)
+        nc.scalar.activation(warm_out[:], w_plane[:, 0:32].bitcast(F32), COPY)
         for q in range(4):
             nc.sync.dma_start(w_plane[32 * q : 32 * q + 4, :].bitcast(I32), w_scales[0, 4 * q : 4 * q + 4, :].bitcast(I32))
         nc.sync.dma_start(w_codes[:].bitcast(I32), w_words[0].rearrange("p m r -> p (m r)").bitcast(I32))
@@ -52,13 +54,13 @@ def tile_picked_hash_lin_none_sub_l_kernel(tc, xT, w_words, w_scales, offs, out)
         left = keep.tile([P, 2 * 2 * V], BF16, name="left", align_bytes=256)
         right = keep.tile([P, 2 * V], F32, name="right", align_bytes=256)
 
-        def gather_even(u):
-            nc.vector.tensor_copy(even[u][0][:], plane[2 * u][:].indirect(entries(0, 0, V)))
-            nc.scalar.activation(even[u][1][:], plane[2 * u][:].indirect(entries(1, 0, V)), COPY)
+        def gather_even(u, v0, v1):
+            nc.vector.tensor_copy(even[u][0][:, v0:v1], plane[2 * u][:].indirect(entries(0, v0, v1)))
+            nc.scalar.activation(even[u][1][:, v0:v1], plane[2 * u][:].indirect(entries(1, v0, v1)), COPY)
 
-        def sum_even(u):
-            halves = [even[u][d][:].bitcast(BF16)[:, 1 : 2 * V] for d in range(D)]
-            nc.vector.tensor_tensor(left[:, 2 * V * u : 2 * V * (u + 1) - 1], halves[0], halves[1], ADD)
+        def sum_even(u, v0, v1):
+            halves = [even[u][d][:].bitcast(BF16)[:, 2 * v0 + 1 : 2 * v1] for d in range(D)]
+            nc.vector.tensor_tensor(left[:, 2 * (V * u + v0) : 2 * (V * u + v1) - 1], halves[0], halves[1], ADD)
 
         def gather_odd(u, v0, v1):
             upper = left[:, 2 * (V * u + v0) + 1 : 2 * (V * u + v1) : 2]
@@ -87,9 +89,12 @@ def tile_picked_hash_lin_none_sub_l_kernel(tc, xT, w_words, w_scales, offs, out)
             leave(result[h][:], acc[h][:])
             nc.sync.dma_start(out[:, v0:v1], result[h][:])
 
-        for u in range(2):
-            gather_even(u)
-            sum_even(u)
+        gather_even(0, 0, V)
+        sum_even(0, 0, V)
+        for v0, v1 in HALVES:
+            gather_even(1, v0, v1)
+        for v0, v1 in HALVES:
+            sum_even(1, v0, v1)
         gather_odd(0, 0, V)
         for v0, v1 in HALVES:
             gather_odd(1, v0, v1)

@@ -78,9 +78,9 @@ def tile_picked_hash_lin_none_sub_l_kernel(tc, xT, w_words, w_scales, offs, out)
             nc.vector.tensor_tensor(x_sum[:, 4 * v0 : 4 * v1].rearrange("p (v u e) -> p v u e", u=2, e=2),
                                     sides[0][:, v0:v1], sides[1][:, v0:v1], ADD)
 
-        def quantize(h):
-            v0, v1 = HALVES[h]
-            nc.vector.quantize_mx(out=x_codes[h][:].bitcast(FP8X4), scales=x_plane[h][:], in_=x_sum[:, 4 * v0 : 4 * v1])
+        def quantize(v0, v1):
+            h, c0, c1 = v0 // HALF, v0 % HALF, (v1 - 1) % HALF + 1
+            nc.vector.quantize_mx(out=x_codes[h][:, c0:c1].bitcast(FP8X4), scales=x_plane[h][:, c0:c1], in_=x_sum[:, 4 * v0 : 4 * v1])
 
         def finish(h, leave):
             v0, v1 = HALVES[h]
@@ -98,9 +98,10 @@ def tile_picked_hash_lin_none_sub_l_kernel(tc, xT, w_words, w_scales, offs, out)
         gather_odd(0, 0, V)
         for v0, v1 in HALVES:
             gather_odd(1, v0, v1)
-        for v0, v1 in HALVES:
+        pieces = [(0, HALF), (HALF, HALF + HALF // 2), (HALF + HALF // 2, V)]
+        for v0, v1 in pieces:
             add(v0, v1)
-        quantize(0)
-        quantize(1)
-        finish(0, nc.scalar.copy)
+        for v0, v1 in pieces:
+            quantize(v0, v1)
+        finish(0, nc.vector.tensor_copy)
         finish(1, nc.vector.tensor_copy)

@@ -36,7 +36,8 @@ def tile_picked_hash_lin_none_sub_l_kernel(tc, xT, w_words, w_scales, offs, out)
         plane = [keep.tile([P, T], F32, name="plane%d" % t, align_bytes=4096) for t in range(4)]
         for t in (0, 2, 1):
             nc.sync.dma_start(plane[t][:, : T // 2], x_rows[:, t, : T // 2])
-            nc.scalar.dma_start(plane[t][:, T // 2 :], x_rows[:, t, T // 2 :])
+            second = nc.sync if t == 1 else nc.scalar
+            second.dma_start(plane[t][:, T // 2 :], x_rows[:, t, T // 2 :])
             if t == 0:
                 nc.sync.dma_start(offsets[:], offs)
         nc.sync.dma_start(plane[3][:], x_rows[:, 3, :])
@@ -58,13 +59,15 @@ def tile_picked_hash_lin_none_sub_l_kernel(tc, xT, w_words, w_scales, offs, out)
             nc.vector.tensor_copy(even[u][0][:, v0:v1], plane[2 * u][:].indirect(entries(0, v0, v1)))
             nc.scalar.activation(even[u][1][:, v0:v1], plane[2 * u][:].indirect(entries(1, v0, v1)), COPY)
 
-        def sum_even(u, v0, v1):
-            halves = [even[u][d][:].bitcast(BF16)[:, 2 * v0 + 1 : 2 * v1] for d in range(D)]
-            nc.vector.tensor_tensor(left[:, 2 * (V * u + v0) : 2 * (V * u + v1) - 1], halves[0], halves[1], ADD)
+        def sum_even(u, v0, v1, lead=0):
+            halves = [even[u][d][:].bitcast(BF16)[:, 2 * v0 + 1 - lead : 2 * v1] for d in range(D)]
+            nc.vector.tensor_tensor(left[:, 2 * (V * u + v0) - lead : 2 * (V * u + v1) - 1], halves[0], halves[1], ADD)
 
-        def gather_odd(u, v0, v1):
+        def gather_odd_left(u, v0, v1):
             upper = left[:, 2 * (V * u + v0) + 1 : 2 * (V * u + v1) : 2]
             nc.vector.tensor_copy(upper, plane[2 * u + 1][:].indirect(entries(0, v0, v1)))
+
+        def gather_odd_right(u, v0, v1):
             nc.scalar.activation(right[:, V * u + v0 : V * u + v1], plane[2 * u + 1][:].indirect(entries(1, v0, v1)), COPY)
 
         x_sum = keep.tile([P, 4 * V], BF16, name="x_sum", align_bytes=256)
@@ -91,13 +94,16 @@ def tile_picked_hash_lin_none_sub_l_kernel(tc, xT, w_words, w_scales, offs, out)
 
         gather_even(0, 0, V)
         sum_even(0, 0, V)
-        for v0, v1 in HALVES:
+        for v0, v1 in reversed(HALVES):
             gather_even(1, v0, v1)
+        sum_even(1, HALF, V)
+        sum_even(1, 0, HALF, lead=1)
         for v0, v1 in HALVES:
-            sum_even(1, v0, v1)
-        gather_odd(0, 0, V)
+            gather_odd_left(0, v0, v1)
+        gather_odd_right(0, 0, V)
         for v0, v1 in HALVES:
-            gather_odd(1, v0, v1)
+            gather_odd_left(1, v0, v1)
+            gather_odd_right(1, v0, v1)
         pieces = [(0, HALF), (HALF, HALF + HALF // 2), (HALF + HALF // 2, V)]
         for v0, v1 in pieces:
             add(v0, v1)

@@ -36,7 +36,7 @@ def tile_picked_hash_lin_none_sub_l_kernel(tc, xT, w_words, w_scales, offs, out)
         plane = [keep.tile([P, T], F32, name="plane%d" % t, align_bytes=4096) for t in range(4)]
         for t in (0, 2, 1):
             nc.sync.dma_start(plane[t][:, : T // 2], x_rows[:, t, : T // 2])
-            second = nc.sync if t == 1 else nc.scalar
+            second = nc.scalar if t == 0 else nc.sync
             second.dma_start(plane[t][:, T // 2 :], x_rows[:, t, T // 2 :])
             if t == 0:
                 nc.sync.dma_start(offsets[:], offs)

@@ -18,7 +18,11 @@ COPY = mybir.ActivationFunctionType.Copy
 P = 128
 S = D * V
 HALF = V // 2
+QUARTER = V // 4
 HALVES = [(0, HALF), (HALF, V)]
+PARTS = [(0, HALF), (HALF, HALF + QUARTER), (HALF + QUARTER, V)]
+PLANE_ORDER = (0, 2, 1, 3)
+ALIGN = 256
 
 
 def tile_picked_hash_lin_none_sub_l_kernel(tc, xT, w_words, w_scales, offs, out):
@@ -29,39 +33,41 @@ def tile_picked_hash_lin_none_sub_l_kernel(tc, xT, w_words, w_scales, offs, out)
         keep = ctx.enter_context(tc.tile_pool(name="keep", bufs=1))
         psum = ctx.enter_context(tc.psum_pool(name="psum", bufs=1))
 
-        offsets = keep.tile([P, S // 16], U16, name="offsets", align_bytes=256)
-        w_codes = keep.tile([P, N], U32, name="w_codes", align_bytes=256)
-        w_plane = keep.tile([P, N], U8, name="w_plane", align_bytes=256)
+        offsets = keep.tile([P, S // 16], U16, name="offsets", align_bytes=ALIGN)
+        w_codes = keep.tile([P, N], U32, name="w_codes", align_bytes=ALIGN)
+        w_scale = keep.tile([P, N], U8, name="w_scale", align_bytes=ALIGN)
         warm_out = keep.tile([P, 8], BF16, name="warm_out")
-        plane = [keep.tile([P, T], F32, name="plane%d" % t, align_bytes=4096) for t in range(4)]
-        for t in (0, 2, 1):
-            nc.sync.dma_start(plane[t][:, : T // 2], x_rows[:, t, : T // 2])
-            second = nc.scalar if t == 0 else nc.sync
-            second.dma_start(plane[t][:, T // 2 :], x_rows[:, t, T // 2 :])
-            if t == 0:
-                nc.sync.dma_start(offsets[:], offs)
-        nc.sync.dma_start(plane[3][:], x_rows[:, 3, :])
+        plane = [keep.tile([P, T], F32, name="plane%d" % t, align_bytes=4 * T) for t in range(4)]
 
-        nc.vector.memset(w_plane[:].bitcast(U32), 0)
-        nc.scalar.activation(warm_out[:], w_plane[:, 0:32].bitcast(F32), COPY)
+        first, *middle, last = PLANE_ORDER
+        nc.sync.dma_start(plane[first][:, : T // 2], x_rows[:, first, : T // 2])
+        nc.scalar.dma_start(plane[first][:, T // 2 :], x_rows[:, first, T // 2 :])
+        nc.sync.dma_start(offsets[:], offs)
+        for t in middle:
+            nc.sync.dma_start(plane[t][:, : T // 2], x_rows[:, t, : T // 2])
+            nc.sync.dma_start(plane[t][:, T // 2 :], x_rows[:, t, T // 2 :])
+        nc.sync.dma_start(plane[last][:], x_rows[:, last, :])
+
+        nc.vector.memset(w_scale[:].bitcast(U32), 0)
+        nc.scalar.activation(warm_out[:], w_scale[:, 0:32].bitcast(F32), COPY)
         for q in range(4):
-            nc.sync.dma_start(w_plane[32 * q : 32 * q + 4, :].bitcast(I32), w_scales[0, 4 * q : 4 * q + 4, :].bitcast(I32))
+            nc.sync.dma_start(w_scale[32 * q : 32 * q + 4, :].bitcast(I32), w_scales[0, 4 * q : 4 * q + 4, :].bitcast(I32))
         nc.sync.dma_start(w_codes[:].bitcast(I32), w_words[0].rearrange("p m r -> p (m r)").bitcast(I32))
 
         def entries(d, v0, v1):
             return offsets[:, (V * d + v0) // 16 : (V * d + v1) // 16]
 
-        even = [[keep.tile([P, V], F32, name="even%d_%d" % (u, d), align_bytes=256) for d in range(D)] for u in range(2)]
-        left = keep.tile([P, 2 * 2 * V], BF16, name="left", align_bytes=256)
-        right = keep.tile([P, 2 * V], F32, name="right", align_bytes=256)
+        even = [keep.tile([P, 2 * V], F32, name="even%d" % d, align_bytes=ALIGN) for d in range(D)]
+        left = keep.tile([P, 2 * 2 * V], BF16, name="left", align_bytes=ALIGN)
+        right = keep.tile([P, 2 * V], F32, name="right", align_bytes=ALIGN)
 
         def gather_even(u, v0, v1):
-            nc.vector.tensor_copy(even[u][0][:, v0:v1], plane[2 * u][:].indirect(entries(0, v0, v1)))
-            nc.scalar.activation(even[u][1][:, v0:v1], plane[2 * u][:].indirect(entries(1, v0, v1)), COPY)
+            nc.vector.tensor_copy(even[0][:, V * u + v0 : V * u + v1], plane[2 * u][:].indirect(entries(0, v0, v1)))
+            nc.scalar.activation(even[1][:, V * u + v0 : V * u + v1], plane[2 * u][:].indirect(entries(1, v0, v1)), COPY)
 
-        def sum_even(u, v0, v1, lead=0):
-            halves = [even[u][d][:].bitcast(BF16)[:, 2 * v0 + 1 - lead : 2 * v1] for d in range(D)]
-            nc.vector.tensor_tensor(left[:, 2 * (V * u + v0) - lead : 2 * (V * u + v1) - 1], halves[0], halves[1], ADD)
+        def sum_even(c0, c1):
+            shifted = [even[d][:].bitcast(BF16)[:, 2 * c0 + 1 : 2 * c1] for d in range(D)]
+            nc.vector.tensor_tensor(left[:, 2 * c0 : 2 * c1 - 1], shifted[0], shifted[1], ADD)
 
         def gather_odd_left(u, v0, v1):
             upper = left[:, 2 * (V * u + v0) + 1 : 2 * (V * u + v1) : 2]
@@ -70,44 +76,45 @@ def tile_picked_hash_lin_none_sub_l_kernel(tc, xT, w_words, w_scales, offs, out)
         def gather_odd_right(u, v0, v1):
             nc.scalar.activation(right[:, V * u + v0 : V * u + v1], plane[2 * u + 1][:].indirect(entries(1, v0, v1)), COPY)
 
-        x_sum = keep.tile([P, 4 * V], BF16, name="x_sum", align_bytes=256)
-        x_codes = [keep.tile([P, HALF], U32, name="x_codes%d" % h, align_bytes=256) for h in range(2)]
-        x_plane = [keep.tile([P, HALF], U8, name="x_plane%d" % h, align_bytes=256) for h in range(2)]
-        acc = [psum.tile([P, HALF], F32, name="acc%d" % h) for h in range(2)]
-        result = [keep.tile([P, HALF], F32, name="result%d" % h, align_bytes=256) for h in range(2)]
+        x_sum = keep.tile([P, 4 * V], BF16, name="x_sum", align_bytes=ALIGN)
+        x_codes = [keep.tile([P, v1 - v0], U32, name="x_codes%d" % v0, align_bytes=ALIGN) for v0, v1 in PARTS]
+        x_scale = [keep.tile([P, v1 - v0], U8, name="x_scale%d" % v0, align_bytes=ALIGN) for v0, v1 in PARTS]
+        acc = [psum.tile([P, v1 - v0], F32, name="acc%d" % v0) for v0, v1 in PARTS]
+        result = [keep.tile([P, HALF], F32, name="result%d" % h, align_bytes=ALIGN) for h in range(len(HALVES))]
 
         def add(v0, v1):
             sides = [side.rearrange("p (u v e) -> p v u e", u=2, e=2) for side in (left[:], right[:].bitcast(BF16))]
             nc.vector.tensor_tensor(x_sum[:, 4 * v0 : 4 * v1].rearrange("p (v u e) -> p v u e", u=2, e=2),
                                     sides[0][:, v0:v1], sides[1][:, v0:v1], ADD)
 
-        def quantize(v0, v1):
-            h, c0, c1 = v0 // HALF, v0 % HALF, (v1 - 1) % HALF + 1
-            nc.vector.quantize_mx(out=x_codes[h][:, c0:c1].bitcast(FP8X4), scales=x_plane[h][:, c0:c1], in_=x_sum[:, 4 * v0 : 4 * v1])
+        def quantize(part):
+            v0, v1 = PARTS[part]
+            nc.vector.quantize_mx(out=x_codes[part][:].bitcast(FP8X4), scales=x_scale[part][:], in_=x_sum[:, 4 * v0 : 4 * v1])
 
-        def finish(h, leave):
-            v0, v1 = HALVES[h]
-            nc.tensor.matmul_mx(out=acc[h][:], lhsT=w_codes[:].bitcast(FP8X4), lhsT_scale=w_plane[:],
-                                rhs=x_codes[h][:].bitcast(FP8X4), rhs_scale=x_plane[h][:], start=True, stop=True)
-            leave(result[h][:], acc[h][:])
-            nc.sync.dma_start(out[:, v0:v1], result[h][:])
+        def multiply(part):
+            v0, v1 = PARTS[part]
+            nc.tensor.matmul_mx(out=acc[part][:], lhsT=w_codes[:].bitcast(FP8X4), lhsT_scale=w_scale[:],
+                                rhs=x_codes[part][:].bitcast(FP8X4), rhs_scale=x_scale[part][:], start=True, stop=True)
+            nc.vector.tensor_copy(result[v0 // HALF][:, v0 % HALF : v0 % HALF + v1 - v0], acc[part][:])
 
         gather_even(0, 0, V)
-        sum_even(0, 0, V)
+        sum_even(0, V - QUARTER)
         for v0, v1 in reversed(HALVES):
             gather_even(1, v0, v1)
-        sum_even(1, HALF, V)
-        sum_even(1, 0, HALF, lead=1)
+        sum_even(V + HALF, 2 * V)
+        sum_even(V - QUARTER, V + HALF)
         for v0, v1 in HALVES:
             gather_odd_left(0, v0, v1)
         gather_odd_right(0, 0, V)
         for v0, v1 in HALVES:
             gather_odd_left(1, v0, v1)
             gather_odd_right(1, v0, v1)
-        pieces = [(0, HALF), (HALF, HALF + HALF // 2), (HALF + HALF // 2, V)]
-        for v0, v1 in pieces:
+
+        for v0, v1 in PARTS:
             add(v0, v1)
-        for v0, v1 in pieces:
-            quantize(v0, v1)
-        finish(0, nc.vector.tensor_copy)
-        finish(1, nc.vector.tensor_copy)
+        for part in range(len(PARTS)):
+            quantize(part)
+        for part in range(len(PARTS)):
+            multiply(part)
+        for h, (v0, v1) in enumerate(HALVES):
+            nc.sync.dma_start(out[:, v0:v1], result[h][:])

@@ -21,7 +21,7 @@ HALF = V // 2
 QUARTER = V // 4
 HALVES = [(0, HALF), (HALF, V)]
 PARTS = [(0, HALF), (HALF, HALF + QUARTER), (HALF + QUARTER, V)]
-PLANE_ORDER = (0, 2, 1, 3)
+PLANE_ORDER = (3, 1, 0, 2)
 ALIGN = 256
 
 
@@ -54,27 +54,16 @@ def tile_picked_hash_lin_none_sub_l_kernel(tc, xT, w_words, w_scales, offs, out)
             nc.sync.dma_start(w_scale[32 * q : 32 * q + 4, :].bitcast(I32), w_scales[0, 4 * q : 4 * q + 4, :].bitcast(I32))
         nc.sync.dma_start(w_codes[:].bitcast(I32), w_words[0].rearrange("p m r -> p (m r)").bitcast(I32))
 
-        def entries(d, v0, v1):
-            return offsets[:, (V * d + v0) // 16 : (V * d + v1) // 16]
+        picked = [keep.tile([P, 2 * V], F32, name="picked%d" % d, align_bytes=ALIGN) for d in range(D)]
 
-        even = [keep.tile([P, 2 * V], F32, name="even%d" % d, align_bytes=ALIGN) for d in range(D)]
-        left = keep.tile([P, 2 * 2 * V], BF16, name="left", align_bytes=ALIGN)
-        right = keep.tile([P, 2 * V], F32, name="right", align_bytes=ALIGN)
-
-        def gather_even(u, v0, v1):
-            nc.vector.tensor_copy(even[0][:, V * u + v0 : V * u + v1], plane[2 * u][:].indirect(entries(0, v0, v1)))
-            nc.scalar.activation(even[1][:, V * u + v0 : V * u + v1], plane[2 * u][:].indirect(entries(1, v0, v1)), COPY)
-
-        def sum_even(c0, c1):
-            shifted = [even[d][:].bitcast(BF16)[:, 2 * c0 + 1 : 2 * c1] for d in range(D)]
-            nc.vector.tensor_tensor(left[:, 2 * c0 : 2 * c1 - 1], shifted[0], shifted[1], ADD)
-
-        def gather_odd_left(u, v0, v1):
-            upper = left[:, 2 * (V * u + v0) + 1 : 2 * (V * u + v1) : 2]
-            nc.vector.tensor_copy(upper, plane[2 * u + 1][:].indirect(entries(0, v0, v1)))
-
-        def gather_odd_right(u, v0, v1):
-            nc.scalar.activation(right[:, V * u + v0 : V * u + v1], plane[2 * u + 1][:].indirect(entries(1, v0, v1)), COPY)
+        def gather(t, d, v0, v1, on_vector):
+            words = picked[d][:, V * (t // 2) + v0 : V * (t // 2) + v1]
+            target = words if t % 2 else words.bitcast(BF16)[:, 0 : 2 * (v1 - v0) : 2]
+            source = plane[t][:].indirect(offsets[:, (V * d + v0) // 16 : (V * d + v1) // 16])
+            if on_vector:
+                nc.vector.tensor_copy(target, source)
+            else:
+                nc.scalar.activation(target, source, COPY)
 
         x_sum = keep.tile([P, 4 * V], BF16, name="x_sum", align_bytes=ALIGN)
         x_codes = [keep.tile([P, v1 - v0], U32, name="x_codes%d" % v0, align_bytes=ALIGN) for v0, v1 in PARTS]
@@ -83,7 +72,7 @@ def tile_picked_hash_lin_none_sub_l_kernel(tc, xT, w_words, w_scales, offs, out)
         result = [keep.tile([P, HALF], F32, name="result%d" % h, align_bytes=ALIGN) for h in range(len(HALVES))]
 
         def add(v0, v1):
-            sides = [side.rearrange("p (u v e) -> p v u e", u=2, e=2) for side in (left[:], right[:].bitcast(BF16))]
+            sides = [side[:].bitcast(BF16).rearrange("p (u v e) -> p v u e", u=2, e=2) for side in picked]
             nc.vector.tensor_tensor(x_sum[:, 4 * v0 : 4 * v1].rearrange("p (v u e) -> p v u e", u=2, e=2),
                                     sides[0][:, v0:v1], sides[1][:, v0:v1], ADD)
 
@@ -97,18 +86,12 @@ def tile_picked_hash_lin_none_sub_l_kernel(tc, xT, w_words, w_scales, offs, out)
                                 rhs=x_codes[part][:].bitcast(FP8X4), rhs_scale=x_scale[part][:], start=True, stop=True)
             nc.vector.tensor_copy(result[v0 // HALF][:, v0 % HALF : v0 % HALF + v1 - v0], acc[part][:])
 
-        gather_even(0, 0, V)
-        sum_even(0, V - QUARTER)
-        for v0, v1 in reversed(HALVES):
-            gather_even(1, v0, v1)
-        sum_even(V + HALF, 2 * V)
-        sum_even(V - QUARTER, V + HALF)
+        for t in PLANE_ORDER[:-1]:
+            gather(t, 0, 0, V, True)
+            gather(t, 1, 0, V, False)
         for v0, v1 in HALVES:
-            gather_odd_left(0, v0, v1)
-        gather_odd_right(0, 0, V)
-        for v0, v1 in HALVES:
-            gather_odd_left(1, v0, v1)
-            gather_odd_right(1, v0, v1)
+            gather(last, 0, v0, v1, True)
+            gather(last, 1, v0, v1, False)
 
         for v0, v1 in PARTS:
             add(v0, v1)

@@ -46,7 +46,7 @@ def tile_picked_hash_lin_none_sub_l_kernel(tc, xT, w_words, w_scales, offs, out)
         for t in middle:
             nc.sync.dma_start(plane[t][:, : T // 2], x_rows[:, t, : T // 2])
             nc.sync.dma_start(plane[t][:, T // 2 :], x_rows[:, t, T // 2 :])
-        nc.sync.dma_start(plane[last][:], x_rows[:, last, :])
+        nc.sync.dma_start(plane[last][:], x_rows[:, last, :], max_dma_last_dim=2048)
 
         nc.vector.memset(w_scale[:].bitcast(U32), 0)
         nc.scalar.activation(warm_out[:], w_scale[:, 0:32].bitcast(F32), COPY)

from contextlib import ExitStack

import concourse.mybir as mybir

K, T, D, V, N = 512, 1024, 2, 256, 128
FLOPS = 2 * K * V * N

F32 = mybir.dt.float32
BF16 = mybir.dt.bfloat16
I32 = mybir.dt.int32
U32 = mybir.dt.uint32
U16 = mybir.dt.uint16
U8 = mybir.dt.uint8
FP8X4 = mybir.dt.float8_e4m3fn_x4
ADD = mybir.AluOpType.add
COPY = mybir.ActivationFunctionType.Copy

P = 128
S = D * V
HALF = V // 2
QUARTER = V // 4
HALVES = [(0, HALF), (HALF, V)]
PARTS = [(0, HALF), (HALF, HALF + QUARTER), (HALF + QUARTER, V)]
PLANE_ORDER = (3, 1, 0, 2)
ALIGN = 256


def tile_picked_hash_lin_none_sub_l_kernel(tc, xT, w_words, w_scales, offs, out):
    nc = tc.nc
    x_rows = xT.rearrange("(p t) c -> p t c", t=4)

    with ExitStack() as ctx:
        keep = ctx.enter_context(tc.tile_pool(name="keep", bufs=1))
        psum = ctx.enter_context(tc.psum_pool(name="psum", bufs=1))

        offsets = keep.tile([P, S // 16], U16, name="offsets", align_bytes=ALIGN)
        w_codes = keep.tile([P, N], U32, name="w_codes", align_bytes=ALIGN)
        w_scale = keep.tile([P, N], U8, name="w_scale", align_bytes=ALIGN)
        warm_out = keep.tile([P, 8], BF16, name="warm_out")
        plane = [keep.tile([P, T], F32, name="plane%d" % t, align_bytes=4 * T) for t in range(4)]

        first, *middle, last = PLANE_ORDER
        nc.sync.dma_start(plane[first][:, : T // 2], x_rows[:, first, : T // 2])
        nc.scalar.dma_start(plane[first][:, T // 2 :], x_rows[:, first, T // 2 :])
        nc.sync.dma_start(offsets[:], offs)
        for t in middle:
            nc.sync.dma_start(plane[t][:, : T // 2], x_rows[:, t, : T // 2])
            nc.sync.dma_start(plane[t][:, T // 2 :], x_rows[:, t, T // 2 :])
        nc.sync.dma_start(plane[last][:], x_rows[:, last, :], max_dma_last_dim=2048)

        nc.vector.memset(w_scale[:].bitcast(U32), 0)
        nc.scalar.activation(warm_out[:], w_scale[:, 0:32].bitcast(F32), COPY)
        for q in range(4):
            nc.sync.dma_start(w_scale[32 * q : 32 * q + 4, :].bitcast(I32), w_scales[0, 4 * q : 4 * q + 4, :].bitcast(I32))
        nc.sync.dma_start(w_codes[:].bitcast(I32), w_words[0].rearrange("p m r -> p (m r)").bitcast(I32))

        picked = [keep.tile([P, 2 * V], F32, name="picked%d" % d, align_bytes=ALIGN) for d in range(D)]

        def gather(t, d, v0, v1, on_vector):
            words = picked[d][:, V * (t // 2) + v0 : V * (t // 2) + v1]
            target = words if t % 2 else words.bitcast(BF16)[:, 0 : 2 * (v1 - v0) : 2]
            source = plane[t][:].indirect(offsets[:, (V * d + v0) // 16 : (V * d + v1) // 16])
            if on_vector:
                nc.vector.tensor_copy(target, source)
            else:
                nc.scalar.activation(target, source, COPY)

        x_sum = keep.tile([P, 4 * V], BF16, name="x_sum", align_bytes=ALIGN)
        x_codes = [keep.tile([P, v1 - v0], U32, name="x_codes%d" % v0, align_bytes=ALIGN) for v0, v1 in PARTS]
        x_scale = [keep.tile([P, v1 - v0], U8, name="x_scale%d" % v0, align_bytes=ALIGN) for v0, v1 in PARTS]
        acc = [psum.tile([P, v1 - v0], F32, name="acc%d" % v0) for v0, v1 in PARTS]
        result = [keep.tile([P, HALF], F32, name="result%d" % h, align_bytes=ALIGN) for h in range(len(HALVES))]

        def add(v0, v1):
            sides = [side[:].bitcast(BF16).rearrange("p (u v e) -> p v u e", u=2, e=2) for side in picked]
            nc.vector.tensor_tensor(x_sum[:, 4 * v0 : 4 * v1].rearrange("p (v u e) -> p v u e", u=2, e=2),
                                    sides[0][:, v0:v1], sides[1][:, v0:v1], ADD)

        def quantize(part):
            v0, v1 = PARTS[part]
            nc.vector.quantize_mx(out=x_codes[part][:].bitcast(FP8X4), scales=x_scale[part][:], in_=x_sum[:, 4 * v0 : 4 * v1])

        def multiply(part):
            v0, v1 = PARTS[part]
            nc.tensor.matmul_mx(out=acc[part][:], lhsT=w_codes[:].bitcast(FP8X4), lhsT_scale=w_scale[:],
                                rhs=x_codes[part][:].bitcast(FP8X4), rhs_scale=x_scale[part][:], start=True, stop=True)
            nc.vector.tensor_copy(result[v0 // HALF][:, v0 % HALF : v0 % HALF + v1 - v0], acc[part][:])

        for t in PLANE_ORDER[:-1]:
            gather(t, 0, 0, V, True)
            gather(t, 1, 0, V, False)
        for v0, v1 in HALVES:
            gather(last, 0, v0, v1, True)
            gather(last, 1, v0, v1, False)

        for v0, v1 in PARTS:
            add(v0, v1)
        for part in range(len(PARTS)):
            quantize(part)
        for part in range(len(PARTS)):
            multiply(part)
        for h, (v0, v1) in enumerate(HALVES):
            nc.sync.dma_start(out[:, v0:v1], result[h][:])
